import numpy as np
import ml_dtypes


def mxq(x, axis, fmt="e4m3"):
    dtype, down = {"e4m3": (ml_dtypes.float8_e4m3fn, 7), "e5m2": (ml_dtypes.float8_e5m2, 14)}[fmt]
    v = np.moveaxis(np.asarray(x, np.float32).astype(ml_dtypes.bfloat16).astype(np.float64), axis, -1)
    blocks = v.reshape(v.shape[:-1] + (-1, 32))
    amax = np.abs(blocks).max(-1, keepdims=True)
    byte = np.maximum(np.where(amax > 0, np.frexp(amax)[1] - 1 + 127, 0) - down, 1)
    scale = np.exp2(byte - 127.0)
    codes = (blocks / scale).astype(np.float32).astype(dtype).astype(np.float64)
    return np.moveaxis((codes * scale).reshape(v.shape), -1, axis)


WIDE = False


def mx_kscale(k):
    if not WIDE:
        return np.ones(k)
    levels = np.array([10, -10, 5, -5, 0])
    if k % 512:
        return np.exp2(np.random.permutation(np.resize(levels, k // 32))).repeat(32)
    a = np.empty((k // 512, 16))
    for p in range(k // 512):
        a[p, :8] = np.random.permutation(np.resize(levels, 8))
        for g in range(8):
            far = levels[np.abs(levels - a[p, g]) >= 10]
            a[p, g + 8] = far[np.random.randint(len(far))]
    return np.exp2(a.ravel()).repeat(32)


def f64(x):
    return np.asarray(x).astype(np.float64)


def striped(idx):
    return np.tile(idx.reshape(-1, 16).T, (8, 1)).astype(np.uint16)


def unstriped(offs):
    return offs[:16].T.reshape(-1).astype(np.int64)


E2M1 = np.array([0.0, 0.5, 1.0, 1.5, 2.0, 3.0, 4.0, 6.0, -0.0, -0.5, -1.0, -1.5, -2.0, -3.0, -4.0, -6.0])


def pack_weight(w, fmt):
    k, n = w.shape
    w = f64(np.asarray(w, np.float32).astype(ml_dtypes.bfloat16)).reshape(k // 32, 32, n)
    amax = np.abs(w).max(1)
    if fmt == "e4m3":
        byte = np.frexp(amax)[1] - 1 + 127 - 7
    else:
        mant, ex = np.frexp(amax / 6.0)
        byte = np.where(mant > 0.5, ex, ex - 1) + 127
    byte = np.clip(np.where(amax > 0, byte, 1), 1, 254)
    scaled = (w * np.exp2(127.0 - byte)[:, None, :]).reshape(k, n).astype(np.float32)
    by_word = np.ascontiguousarray(scaled.reshape(k // 512, 128, 4, n).transpose(0, 1, 3, 2))
    if fmt == "e4m3":
        words = by_word.astype(ml_dtypes.float8_e4m3fn).view(np.uint8)
    else:
        c = by_word.astype(ml_dtypes.float4_e2m1fn).view(np.uint8) & 0xF
        words = (c[..., 0::2] | (c[..., 1::2] << 4)).reshape(k // 512, 128, 2 * n)
    return np.ascontiguousarray(words), np.ascontiguousarray(byte.astype(np.uint8).reshape(k // 512, 16, n))


def unpack_weight(words, scales, fmt):
    g, _, n = scales.shape
    words = np.ascontiguousarray(words).reshape(g, 128, n, -1)
    if fmt == "e4m3":
        vals = words.view(ml_dtypes.float8_e4m3fn).astype(np.float64)
    else:
        nib = np.empty((g, 128, n, 4), np.uint8)
        nib[..., 0::2] = words & 0xF
        nib[..., 1::2] = words >> 4
        vals = E2M1[nib]
    vals = vals * np.repeat(np.exp2(scales.astype(np.float64) - 127.0), 8, axis=1)[..., None]
    return vals.transpose(0, 1, 3, 2).reshape(g * 512, n)


def gelu(v):
    return 0.5 * v * (1.0 + np.tanh(np.sqrt(2.0 / np.pi) * (v + 0.044715 * v**3)))


K, KA, T, H, S, S2, T3, P = 1024, 512, 4096, 1024, 1024, 1024, 2048, 512


def setup_inputs():
    n = np.random.standard_normal
    s = mx_kscale(K)[:, None]
    u = mx_kscale(H)[:, None]
    tab_words, tab_scales = pack_weight(n((K, T)) * s, "e4m3")
    tab2_words, tab2_scales = pack_weight(1.2 * n((H, T3)) / np.sqrt(H) / u, "e4m3")
    w4_words, w4_scales = pack_weight(1.2 * n((KA, H)) / np.sqrt(K) / s[:KA], "e2m1")
    return {
        "tab_words": tab_words, "tab_scales": tab_scales,
        "offs": striped(np.random.permutation(T)[:S]),
        "tab2_words": tab2_words, "tab2_scales": tab2_scales,
        "offs2": striped(np.random.permutation(T3)[:S2]),
        "pos1": striped(np.random.permutation(S)[:P]),
        "pos2": striped(np.random.permutation(S)[:P]),
        "w4_words": w4_words, "w4_scales": w4_scales,
        "w1": (1.2 * n((K - KA, H)) / np.sqrt(K) / s[KA:]).astype(np.float32),
        "b1": (0.7 * n(H)).astype(np.float32),
        "appetite": n((H, S)).astype(np.float32),
        "gain": (np.exp(0.3 * n(H)) * u[:, 0]).astype(np.float32),
        "late": (0.4 * n(H) * u[:, 0]).astype(np.float32),
        "extra": (0.7 * n((S2, P))).astype(np.float32),
    }


def reference(tab_words, tab_scales, offs, tab2_words, tab2_scales, offs2, pos1, pos2,
              w4_words, w4_scales, w1, b1, appetite, gain, late, extra):
    v = unpack_weight(tab_words, tab_scales, "e4m3")[:, unstriped(offs)]
    v2 = unpack_weight(tab2_words, tab2_scales, "e4m3")[:, unstriped(offs2)]
    w4 = unpack_weight(w4_words, w4_scales, "e2m1")
    q1 = mxq(f64(w1), 0, "e4m3")
    y = w4.T @ v[:KA] + q1.T @ v[KA:]
    h = np.tanh(y + f64(b1)[:, None]) * f64(appetite) * f64(gain)[:, None]
    x1 = mxq(h[:, unstriped(pos1)], 0, "e4m3")
    x2 = mxq(np.maximum(h[:, unstriped(pos2)], f64(late)[:, None]), 0, "e4m3")
    e1 = v2.T @ x1
    e2 = v2.T @ x2
    return np.maximum(e1, e2 + f64(extra))

@@ -1,0 +1,242 @@
+from contextlib import ExitStack
+
+import concourse.mybir as mybir
+
+F32 = mybir.dt.float32
+BF16 = mybir.dt.bfloat16
+I32 = mybir.dt.int32
+U32 = mybir.dt.uint32
+U16 = mybir.dt.uint16
+U8 = mybir.dt.uint8
+E4M3X4 = mybir.dt.float8_e4m3fn_x4
+E2M1X4 = mybir.dt.float4_e2m1fn_x4
+ALU = mybir.AluOpType
+ACT = mybir.ActivationFunctionType
+
+P = 128
+PACK = 4
+PASS = P * PACK
+T, T3, H, S, S2, NP = 4096, 2048, 1024, 1024, 1024, 512
+BANK = 512
+BANKS = 8
+LIST_ROWS = 16
+
+FLOPS = 2 * 1024 * H * S + 2 * 2 * H * S2 * NP
+
+
+def tile_list_breakfast_refill_scores_kernel(
+    tc, tab_words, tab_scales, offs, tab2_words, tab2_scales, offs2, pos1, pos2,
+    w4_words, w4_scales, w1, b1, appetite, gain, late, extra, out,
+):
+    nc = tc.nc
+    with ExitStack() as ctx:
+        lists = ctx.enter_context(tc.tile_pool(name="lists", bufs=1))
+        keep = ctx.enter_context(tc.tile_pool(name="keep", bufs=1))
+        psum = ctx.enter_context(tc.psum_pool(name="psum", bufs=1))
+
+        def load_list(src, name):
+            tile = lists.tile(list(src.shape), U16, name=name)
+            nc.sync.dma_start(tile[:], src)
+            return tile
+
+        def zeroed_plane(engine, width, name, tag):
+            plane = keep.tile([P, width], U8, name=name, tag=tag, align_bytes=64)
+            engine.memset(plane[:].bitcast(I32), 0)
+            return plane
+
+        def load_scale_rows(queue, plane, scales):
+            passes = scales.shape[0]
+            for q in range(4):
+                rows = scales[:, 4 * q : 4 * q + 4, :] if passes > 1 else scales[0, 4 * q : 4 * q + 4, :]
+                queue.dma_start(plane[32 * q : 32 * q + 4 * passes, :].bitcast(I32), rows.bitcast(I32))
+
+        def load_words(words, a, name, tag):
+            tile = keep.tile([P, words.shape[2]], U32, name=name, tag=tag, align_bytes=64)
+            nc.sync.dma_start(tile[:].bitcast(I32), words[a].rearrange("p t i -> p (t i)").bitcast(I32))
+            return tile
+
+        def load_w1(b, tag):
+            raw = keep.tile([P, PACK, PASS], F32, name=f"w1_raw{b}", tag=tag, align_bytes=64)
+            nc.sync.dma_start(raw[:], w1[:, b * PASS : (b + 1) * PASS].rearrange("(p j) c -> p j c", j=PACK))
+            return raw
+
+        def load_appetite(pair, tag):
+            b, t0 = pair // 2, 2 * (pair % 2)
+            tile = keep.tile([P, 2, S], F32, name=f"app{pair}", tag=tag, align_bytes=64)
+            rows = appetite[b * PASS : (b + 1) * PASS, :].rearrange("(p t) j -> p t j", t=PACK)
+            nc.sync.dma_start(tile[:], rows[:, t0 : t0 + 2, :])
+            return tile
+
+        def load_per_row(vec, name):
+            tile = keep.tile([P, 2, PACK], F32, name=name)
+            nc.gpsimd.dma_start(tile[:], vec.rearrange("(b p t) -> p b t", p=P, t=PACK))
+            return tile
+
+        def bank(i, name):
+            return psum.tile([P, BANK], F32, name=name, tag=f"bank{i % BANKS}")
+
+        w4_plane_raw = zeroed_plane(nc.vector, H, "w4_plane_raw", "slot_b")
+        tab_plane = zeroed_plane(nc.vector, T, "tab_plane", "slot_d")
+        tab2_plane = zeroed_plane(nc.gpsimd, T3, "tab2_plane", "slot_f")
+
+        offs_sb = load_list(offs, "offs_sb")
+        w4_raw = keep.tile([P, 2 * H], U8, name="w4_raw", tag="slot_a", align_bytes=64)
+        nc.sync.dma_start(w4_raw[:].bitcast(I32), w4_words[0].bitcast(I32))
+        offs2_sb = load_list(offs2, "offs2_sb")
+        pos2_sb = load_list(pos2, "pos2_sb")
+        pos1_sb = load_list(pos1, "pos1_sb")
+        tab_sb = [load_words(tab_words, 0, "tab0", "slot_c")]
+        load_scale_rows(nc.scalar, w4_plane_raw, w4_scales)
+        load_scale_rows(nc.scalar, tab_plane, tab_scales)
+        load_scale_rows(nc.scalar, tab2_plane, tab2_scales)
+        b1_sb = load_per_row(b1, "b1_sb")
+        gain_sb = load_per_row(gain, "gain_sb")
+        late_sb = load_per_row(late, "late_sb")
+
+        w4 = keep.tile([P, 2 * H], U8, name="w4", align_bytes=64)
+        nc.vector.tensor_copy(
+            w4[:].rearrange("p (b t m e) -> p b t m e", b=2, t=PACK, e=2),
+            w4_raw[:].rearrange("p (b m t e) -> p b t m e", b=2, t=PACK, e=2),
+        )
+        w4_plane = keep.tile([P, H], U8, name="w4_plane", align_bytes=64)
+        nc.vector.tensor_copy(
+            w4_plane[:].rearrange("p (b t m) -> p b t m", b=2, t=PACK),
+            w4_plane_raw[:].rearrange("p (b m t) -> p b t m", b=2, t=PACK),
+        )
+
+        w1_raw = [load_w1(0, "slot_a")]
+        tab_sb.append(load_words(tab_words, 1, "tab1", "slot_b"))
+
+        def quantize(grouped, name):
+            words = keep.tile([P, PASS], U32, name=f"{name}_words", align_bytes=64)
+            plane = keep.tile([P, PASS], U8, name=f"{name}_plane", align_bytes=64)
+            nc.vector.quantize_mx(out=words[:].bitcast(E4M3X4), scales=plane[:], in_=grouped[:])
+            return words, plane
+
+        def round_w1(b):
+            grouped = keep.tile([P, PACK * PASS], BF16, name=f"w1_bf{b}", tag=f"slot_e{b}", align_bytes=64)
+            nc.scalar.copy(
+                grouped[:].rearrange("p (t m j) -> p m t j", t=PACK, j=PACK),
+                w1_raw[b][:].rearrange("p j (m t) -> p m t j", t=PACK),
+            )
+            return grouped
+
+        def gather(dst, window, offsets, pieces):
+            n = dst.shape[1] // pieces
+            for c in range(pieces):
+                cols = offsets[:, c * n // LIST_ROWS : (c + 1) * n // LIST_ROWS]
+                nc.vector.tensor_copy(dst[:, c * n : (c + 1) * n], window[:].indirect(cols))
+
+        v_words = [keep.tile([P, S], U32, name=f"v{a}", align_bytes=64) for a in range(2)]
+        gather(v_words[0], tab_sb[0], offs_sb, 1)
+        tab2_sb = [load_words(tab2_words, 0, "tab2_0", "slot_c")]
+        v_plane = keep.tile([P, S], U8, name="v_plane", align_bytes=64)
+        gather(v_plane, tab_plane, offs_sb, 1)
+        app = [load_appetite(0, "slot_d")]
+        w1_bf = [round_w1(0)]
+        w1_q = [quantize(w1_bf[0], "w1_0")]
+        app.append(load_appetite(1, "slot_e0"))
+        w1_raw.append(load_w1(1, "slot_a"))
+        v2_plane = keep.tile([P, S2], U8, name="v2_plane", align_bytes=64)
+        gather(v2_plane, tab2_plane, offs2_sb, 1)
+        tab2_sb.append(load_words(tab2_words, 1, "tab2_1", "slot_f"))
+        gather(v_words[1], tab_sb[1], offs_sb, 2)
+        app.append(load_appetite(2, "slot_b"))
+        v2_words = [keep.tile([P, S2], U32, name=f"v2_{a}", align_bytes=64) for a in range(2)]
+        gather(v2_words[0], tab2_sb[0], offs2_sb, 1)
+        app.append(load_appetite(3, "slot_c"))
+
+        def first_stage(b, t):
+            h = keep.tile([P, S], F32, name=f"h{b}{t}")
+            w_cols = slice(t * P, (t + 1) * P)
+            c0 = b * PASS + t * P
+            for half in range(S // BANK):
+                cols = slice(half * BANK, (half + 1) * BANK)
+                y = bank(2 * (PACK * b + t) + half, f"y{b}{t}{half}")
+                nc.tensor.matmul_mx(
+                    y[:], lhsT=w4[:, 2 * c0 : 2 * (c0 + P)].bitcast(E2M1X4), lhsT_scale=w4_plane[:, c0 : c0 + P],
+                    rhs=v_words[0][:, cols].bitcast(E4M3X4), rhs_scale=v_plane[:, cols], start=True, stop=False,
+                )
+                nc.tensor.matmul_mx(
+                    y[:], lhsT=w1_q[b][0][:, w_cols].bitcast(E4M3X4), lhsT_scale=w1_q[b][1][:, w_cols],
+                    rhs=v_words[1][:, cols].bitcast(E4M3X4), rhs_scale=v_plane[4:P, cols], start=False, stop=True,
+                )
+                nc.scalar.activation(h[:, cols], y[:], ACT.Tanh, bias=b1_sb[:, b, t : t + 1])
+            return h
+
+        def scale_rows(h, b, t):
+            nc.vector.scalar_tensor_tensor(
+                h[:], h[:], gain_sb[:, b, t : t + 1], app[2 * b + t // 2][:, t % 2, :], ALU.mult, ALU.mult
+            )
+
+        def round_x(picked, name):
+            grouped = keep.tile([P, PACK * NP], BF16, name=name, align_bytes=64)
+            nc.scalar.copy(
+                grouped[:].rearrange("p (c i t) -> p c t i", i=4, t=PACK),
+                picked[:].rearrange("p t (c i) -> p c t i", i=4),
+            )
+            return grouped
+
+        def pick(dst, h, positions):
+            nc.vector.tensor_copy(dst, h[:].indirect(positions[:]))
+
+        def second_stage(acc, i, a, x):
+            nc.tensor.matmul_mx(
+                acc[:], lhsT=v2_words[a][:, i * P : (i + 1) * P].bitcast(E4M3X4),
+                lhsT_scale=v2_plane[4 * a : P, i * P : (i + 1) * P],
+                rhs=x[0][:].bitcast(E4M3X4), rhs_scale=x[1][:], start=(a == 0), stop=(a == 1),
+            )
+
+        h = {}
+        early = [keep.tile([P, PACK, NP], F32, name="early0")]
+        lateb = [keep.tile([P, PACK, NP], F32, name=f"late{b}") for b in range(2)]
+        x1, x2 = [], []
+        for b in range(2):
+            if b == 1:
+                w1_bf.append(round_w1(1))
+                extra_sb = keep.tile([P, S2 // P, NP], F32, name="extra_sb", tag="slot_a", align_bytes=64)
+                nc.sync.dma_start(extra_sb[:], extra.rearrange("(i p) n -> p i n", p=P))
+                w1_q.append(quantize(w1_bf[1], "w1_1"))
+            for t in range(PACK):
+                h[b, t] = first_stage(b, t)
+        for b in range(2):
+            for t in range(PACK):
+                scale_rows(h[b, t], b, t)
+                pick(lateb[b][:, t, :], h[b, t], pos2_sb)
+                if b == 0:
+                    pick(early[0][:, t, :], h[b, t], pos1_sb)
+                nc.vector.tensor_scalar(lateb[b][:, t, :], lateb[b][:, t, :], late_sb[:, b, t : t + 1], None, ALU.max)
+                if (b, t) == (1, 0):
+                    x2.append(quantize(x2_bf, "x2_0"))
+                    gather(v2_words[1], tab2_sb[1], offs2_sb, 1)
+                if (b, t) == (1, 1):
+                    x1.append(quantize(x1_bf, "x1_0"))
+            x2_bf = round_x(lateb[b], f"x2_bf{b}")
+            if b == 0:
+                x1_bf = round_x(early[0], "x1_bf0")
+
+        tiles = S2 // P
+        e2 = [bank(i, f"e2_{i}") for i in range(tiles)]
+        for i in range(tiles):
+            second_stage(e2[i], i, 0, x2[0])
+
+        early.append(keep.tile([P, PACK, NP], F32, name="early1", tag="slot_c", align_bytes=64))
+        for t in range(PACK):
+            pick(early[1][:, t, :], h[1, t], pos1_sb)
+            if t == 1:
+                x2.append(quantize(x2_bf, "x2_1"))
+        for i in range(tiles):
+            second_stage(e2[i], i, 1, x2[1])
+        x1_bf = round_x(early[1], "x1_bf1")
+        e1 = []
+        for i in range(tiles):
+            nc.vector.tensor_tensor(extra_sb[:, i, :], e2[i][:], extra_sb[:, i, :], ALU.add)
+            e1.append(bank(i, f"e1_{i}"))
+            second_stage(e1[i], i, 0, x1[0])
+            if i == 4:
+                x1.append(quantize(x1_bf, "x1_1"))
+        for i in range(tiles):
+            second_stage(e1[i], i, 1, x1[1])
+        for i in range(tiles):
+            nc.vector.tensor_tensor(extra_sb[:, i, :], e1[i][:], extra_sb[:, i, :], ALU.max)
+            nc.sync.dma_start(out[i * P : (i + 1) * P, :], extra_sb[:, i, :])

@@ -19,7 +19,7 @@ PASS = P * PACK
 T, T3, H, S, S2, NP = 4096, 2048, 1024, 1024, 1024, 512
 BANK = 512
 BANKS = 8
-LIST_ROWS = 16
+AT_A, AT_B, AT_C, AT_D = 8, 24, 43, 52
 
 FLOPS = 2 * 1024 * H * S + 2 * 2 * H * S2 * NP
 
@@ -32,15 +32,18 @@ def tile_list_breakfast_refill_scores_kernel(
     with ExitStack() as ctx:
         lists = ctx.enter_context(tc.tile_pool(name="lists", bufs=1))
         keep = ctx.enter_context(tc.tile_pool(name="keep", bufs=1))
+        arena = ctx.enter_context(tc.tile_pool(name="arena", bufs=1))
         psum = ctx.enter_context(tc.psum_pool(name="psum", bufs=1))
+
+        def placed(shape, dtype, name, kib):
+            return arena.tile(shape, dtype, name=name, offset=kib * 1024, align_bytes=64)
 
         def load_list(src, name):
             tile = lists.tile(list(src.shape), U16, name=name)
             nc.sync.dma_start(tile[:], src)
             return tile
 
-        def zeroed_plane(engine, width, name, tag):
-            plane = keep.tile([P, width], U8, name=name, tag=tag, align_bytes=64)
+        def zeroed(engine, plane):
             engine.memset(plane[:].bitcast(I32), 0)
             return plane
 
@@ -50,124 +53,117 @@ def tile_list_breakfast_refill_scores_kernel(
                 rows = scales[:, 4 * q : 4 * q + 4, :] if passes > 1 else scales[0, 4 * q : 4 * q + 4, :]
                 queue.dma_start(plane[32 * q : 32 * q + 4 * passes, :].bitcast(I32), rows.bitcast(I32))
 
-        def load_words(words, a, name, tag):
-            tile = keep.tile([P, words.shape[2]], U32, name=name, tag=tag, align_bytes=64)
+        def load_words(words, a, name, kib):
+            tile = placed([P, words.shape[2]], U32, name, kib)
             nc.sync.dma_start(tile[:].bitcast(I32), words[a].rearrange("p t i -> p (t i)").bitcast(I32))
             return tile
 
-        def load_w1(b, tag):
-            raw = keep.tile([P, PACK, PASS], F32, name=f"w1_raw{b}", tag=tag, align_bytes=64)
-            nc.sync.dma_start(raw[:], w1[:, b * PASS : (b + 1) * PASS].rearrange("(p j) c -> p j c", j=PACK))
-            return raw
 
-        def load_appetite(pair, tag):
+        def load_appetite(pair, kib):
             b, t0 = pair // 2, 2 * (pair % 2)
-            tile = keep.tile([P, 2, S], F32, name=f"app{pair}", tag=tag, align_bytes=64)
+            tile = placed([P, 2, S], F32, f"app{pair}", kib)
             rows = appetite[b * PASS : (b + 1) * PASS, :].rearrange("(p t) j -> p t j", t=PACK)
             nc.sync.dma_start(tile[:], rows[:, t0 : t0 + 2, :])
             return tile
 
-        def load_per_row(vec, name):
-            tile = keep.tile([P, 2, PACK], F32, name=name)
-            nc.gpsimd.dma_start(tile[:], vec.rearrange("(b p t) -> p b t", p=P, t=PACK))
-            return tile
+        def load_per_row(dst, vec):
+            nc.sync.dma_start(dst, vec.rearrange("(b p t) -> p b t", p=P, t=PACK))
+            return dst
 
         def bank(i, name):
             return psum.tile([P, BANK], F32, name=name, tag=f"bank{i % BANKS}")
 
-        w4_plane_raw = zeroed_plane(nc.vector, H, "w4_plane_raw", "slot_b")
-        tab_plane = zeroed_plane(nc.vector, T, "tab_plane", "slot_d")
-        tab2_plane = zeroed_plane(nc.gpsimd, T3, "tab2_plane", "slot_f")
+        def quantize(grouped, name):
+            width = grouped.shape[1] // PACK
+            words = keep.tile([P, width], U32, name=f"{name}_words", align_bytes=64)
+            plane = keep.tile([P, width], U8, name=f"{name}_plane", align_bytes=64)
+            nc.vector.quantize_mx(out=words[:].bitcast(E4M3X4), scales=plane[:], in_=grouped[:])
+            return words, plane
+
+        def round_w1(b, u):
+            grouped = keep.tile([P, 2 * PASS], BF16, name=f"w1_bf{b}{u}", align_bytes=64)
+            nc.scalar.copy(
+                grouped[:].rearrange("p (t m j) -> p m t j", t=2, j=PACK),
+                w1_raw[:, b].rearrange("p j (m t) -> p m t j", t=PACK)[:, :, 2 * u : 2 * u + 2, :],
+            )
+            return grouped
+
+        def gather(dst, window, offsets):
+            nc.vector.tensor_copy(dst, window[:].indirect(offsets[:]))
+
+        tab_plane = zeroed(nc.vector, placed([P, T], U8, "tab_plane", AT_C))
+        w4_plane_raw = zeroed(nc.gpsimd, keep.tile([P, H], U8, name="w4_plane_raw", align_bytes=64))
 
         offs_sb = load_list(offs, "offs_sb")
-        w4_raw = keep.tile([P, 2 * H], U8, name="w4_raw", tag="slot_a", align_bytes=64)
+        w4_raw = placed([P, 2 * H], U8, "w4_raw", AT_A - 1)
         nc.sync.dma_start(w4_raw[:].bitcast(I32), w4_words[0].bitcast(I32))
         offs2_sb = load_list(offs2, "offs2_sb")
         pos2_sb = load_list(pos2, "pos2_sb")
         pos1_sb = load_list(pos1, "pos1_sb")
-        tab_sb = [load_words(tab_words, 0, "tab0", "slot_c")]
-        load_scale_rows(nc.scalar, w4_plane_raw, w4_scales)
+        tab_sb = [load_words(tab_words, 0, "tab0", AT_B)]
         load_scale_rows(nc.scalar, tab_plane, tab_scales)
-        load_scale_rows(nc.scalar, tab2_plane, tab2_scales)
-        b1_sb = load_per_row(b1, "b1_sb")
-        gain_sb = load_per_row(gain, "gain_sb")
-        late_sb = load_per_row(late, "late_sb")
+        load_scale_rows(nc.gpsimd, w4_plane_raw, w4_scales)
 
-        w4 = keep.tile([P, 2 * H], U8, name="w4", align_bytes=64)
+        w4 = keep.tile([P, H], U16, name="w4", align_bytes=64)
         nc.vector.tensor_copy(
-            w4[:].rearrange("p (b t m e) -> p b t m e", b=2, t=PACK, e=2),
-            w4_raw[:].rearrange("p (b m t e) -> p b t m e", b=2, t=PACK, e=2),
+            w4[:].rearrange("p (b t m) -> p b t m", b=2, t=PACK),
+            w4_raw[:].bitcast(U16).rearrange("p (b m t) -> p b t m", b=2, t=PACK),
         )
-        w4_plane = keep.tile([P, H], U8, name="w4_plane", align_bytes=64)
+        w1_raw = placed([P, 2, PACK, PASS], F32, "w1_raw", AT_A)
+        for b in range(2):
+            nc.sync.dma_start(w1_raw[:, b], w1[:, b * PASS : (b + 1) * PASS].rearrange("(p j) c -> p j c", j=PACK))
+        tab2_plane = zeroed(nc.vector, placed([P, T3], U8, "tab2_plane", AT_A - 2))
+        load_scale_rows(nc.scalar, tab2_plane, tab2_scales)
+
+        v_words = [placed([P, S], U32, f"v{a}", AT_D + 4 * a) for a in range(2)]
+        gather(v_words[0][:], tab_sb[0], offs_sb)
+        tab_sb.append(load_words(tab_words, 1, "tab1", AT_B + 3))
+        per_row = placed([P, 3, 2, PACK], F32, "per_row", AT_B + 2)
+        b1_sb, gain_sb, late_sb = [load_per_row(per_row[:, i], vec) for i, vec in enumerate((b1, gain, late))]
+        v_plane = placed([P, S], U8, "v_plane", AT_B)
+        gather(v_plane[:], tab_plane, offs_sb)
+        app = [load_appetite(0, AT_C + 1)]
+        w4_plane = placed([P, H], U8, "w4_plane", AT_B + 1)
         nc.vector.tensor_copy(
             w4_plane[:].rearrange("p (b t m) -> p b t m", b=2, t=PACK),
             w4_plane_raw[:].rearrange("p (b m t) -> p b t m", b=2, t=PACK),
         )
-
-        w1_raw = [load_w1(0, "slot_a")]
-        tab_sb.append(load_words(tab_words, 1, "tab1", "slot_b"))
-
-        def quantize(grouped, name):
-            words = keep.tile([P, PASS], U32, name=f"{name}_words", align_bytes=64)
-            plane = keep.tile([P, PASS], U8, name=f"{name}_plane", align_bytes=64)
-            nc.vector.quantize_mx(out=words[:].bitcast(E4M3X4), scales=plane[:], in_=grouped[:])
-            return words, plane
-
-        def round_w1(b):
-            grouped = keep.tile([P, PACK * PASS], BF16, name=f"w1_bf{b}", tag=f"slot_e{b}", align_bytes=64)
-            nc.scalar.copy(
-                grouped[:].rearrange("p (t m j) -> p m t j", t=PACK, j=PACK),
-                w1_raw[b][:].rearrange("p j (m t) -> p m t j", t=PACK),
-            )
-            return grouped
-
-        def gather(dst, window, offsets, pieces):
-            n = dst.shape[1] // pieces
-            for c in range(pieces):
-                cols = offsets[:, c * n // LIST_ROWS : (c + 1) * n // LIST_ROWS]
-                nc.vector.tensor_copy(dst[:, c * n : (c + 1) * n], window[:].indirect(cols))
-
-        v_words = [keep.tile([P, S], U32, name=f"v{a}", align_bytes=64) for a in range(2)]
-        gather(v_words[0], tab_sb[0], offs_sb, 1)
-        tab2_sb = [load_words(tab2_words, 0, "tab2_0", "slot_c")]
-        v_plane = keep.tile([P, S], U8, name="v_plane", align_bytes=64)
-        gather(v_plane, tab_plane, offs_sb, 1)
-        app = [load_appetite(0, "slot_d")]
-        w1_bf = [round_w1(0)]
-        w1_q = [quantize(w1_bf[0], "w1_0")]
-        app.append(load_appetite(1, "slot_e0"))
-        w1_raw.append(load_w1(1, "slot_a"))
-        v2_plane = keep.tile([P, S2], U8, name="v2_plane", align_bytes=64)
-        gather(v2_plane, tab2_plane, offs2_sb, 1)
-        tab2_sb.append(load_words(tab2_words, 1, "tab2_1", "slot_f"))
-        gather(v_words[1], tab_sb[1], offs_sb, 2)
-        app.append(load_appetite(2, "slot_b"))
+        w1_bf = [round_w1(b, u) for b in range(2) for u in range(2)]
+        app.extend(load_appetite(1 + b, AT_A + 8 * b) for b in range(2))
+        w1_q = [quantize(w1_bf[u], f"w1_0{u}") for u in range(2)]
+        v2_plane = placed([P, S2], U8, "v2_plane", AT_C)
+        gather(v2_plane[:], tab2_plane, offs2_sb)
+        w1_q.extend(quantize(w1_bf[2 + u], f"w1_1{u}") for u in range(2))
+        half_list = offs.shape[1] // 2
+        for half in range(2):
+            cols = slice(half * BANK, (half + 1) * BANK)
+            gather(v_words[1][:, cols], tab_sb[1], offs_sb[:, half * half_list : (half + 1) * half_list])
+        app.append(load_appetite(3, AT_B + 3))
+        tab2_sb = [load_words(tab2_words, 0, "tab2_0", AT_B + 11)]
         v2_words = [keep.tile([P, S2], U32, name=f"v2_{a}", align_bytes=64) for a in range(2)]
-        gather(v2_words[0], tab2_sb[0], offs2_sb, 1)
-        app.append(load_appetite(3, "slot_c"))
 
         def first_stage(b, t):
             h = keep.tile([P, S], F32, name=f"h{b}{t}")
-            w_cols = slice(t * P, (t + 1) * P)
+            w_words, w_plane = w1_q[2 * b + t // 2]
+            w_cols = slice(t % 2 * P, (t % 2 + 1) * P)
             c0 = b * PASS + t * P
             for half in range(S // BANK):
                 cols = slice(half * BANK, (half + 1) * BANK)
                 y = bank(2 * (PACK * b + t) + half, f"y{b}{t}{half}")
                 nc.tensor.matmul_mx(
-                    y[:], lhsT=w4[:, 2 * c0 : 2 * (c0 + P)].bitcast(E2M1X4), lhsT_scale=w4_plane[:, c0 : c0 + P],
+                    y[:], lhsT=w4[:, c0 : c0 + P].bitcast(E2M1X4), lhsT_scale=w4_plane[:, c0 : c0 + P],
                     rhs=v_words[0][:, cols].bitcast(E4M3X4), rhs_scale=v_plane[:, cols], start=True, stop=False,
                 )
                 nc.tensor.matmul_mx(
-                    y[:], lhsT=w1_q[b][0][:, w_cols].bitcast(E4M3X4), lhsT_scale=w1_q[b][1][:, w_cols],
+                    y[:], lhsT=w_words[:, w_cols].bitcast(E4M3X4), lhsT_scale=w_plane[:, w_cols],
                     rhs=v_words[1][:, cols].bitcast(E4M3X4), rhs_scale=v_plane[4:P, cols], start=False, stop=True,
                 )
                 nc.scalar.activation(h[:, cols], y[:], ACT.Tanh, bias=b1_sb[:, b, t : t + 1])
             return h
 
-        def scale_rows(h, b, t):
-            nc.vector.scalar_tensor_tensor(
-                h[:], h[:], gain_sb[:, b, t : t + 1], app[2 * b + t // 2][:, t % 2, :], ALU.mult, ALU.mult
-            )
+        def times_appetite(h, b, t):
+            engine = nc.vector if (b, t) == (0, 0) else nc.gpsimd
+            engine.tensor_tensor(h[:], h[:], app[2 * b + t // 2][:, t % 2, :], ALU.mult)
 
         def round_x(picked, name):
             grouped = keep.tile([P, PACK * NP], BF16, name=name, align_bytes=64)
@@ -176,9 +172,6 @@ def tile_list_breakfast_refill_scores_kernel(
                 picked[:].rearrange("p t (c i) -> p c t i", i=4),
             )
             return grouped
-
-        def pick(dst, h, positions):
-            nc.vector.tensor_copy(dst, h[:].indirect(positions[:]))
 
         def second_stage(acc, i, a, x):
             nc.tensor.matmul_mx(
@@ -189,42 +182,58 @@ def tile_list_breakfast_refill_scores_kernel(
 
         h = {}
         early = [keep.tile([P, PACK, NP], F32, name="early0")]
-        lateb = [keep.tile([P, PACK, NP], F32, name=f"late{b}") for b in range(2)]
+        picked_late = [keep.tile([P, PACK, NP], F32, name=f"late{b}") for b in range(2)]
         x1, x2 = [], []
-        for b in range(2):
-            if b == 1:
-                w1_bf.append(round_w1(1))
-                extra_sb = keep.tile([P, S2 // P, NP], F32, name="extra_sb", tag="slot_a", align_bytes=64)
-                nc.sync.dma_start(extra_sb[:], extra.rearrange("(i p) n -> p i n", p=P))
-                w1_q.append(quantize(w1_bf[1], "w1_1"))
+
+        def times_gain(dst, b, t):
+            nc.scalar.activation(dst[:, t, :], early[b][:, t, :], ACT.Copy, scale=gain_sb[:, b, t : t + 1])
+
+        def floor_late(b, dst):
             for t in range(PACK):
+                nc.vector.tensor_scalar(
+                    dst[:, t, :], picked_late[b][:, t, :], gain_sb[:, b, t : t + 1], late_sb[:, b, t : t + 1],
+                    ALU.mult, ALU.max,
+                )
+            return dst
+
+        for k in range(2 * PACK + 1):
+            if k < 2 * PACK:
+                b, t = divmod(k, PACK)
                 h[b, t] = first_stage(b, t)
-        for b in range(2):
-            for t in range(PACK):
-                scale_rows(h[b, t], b, t)
-                pick(lateb[b][:, t, :], h[b, t], pos2_sb)
+                times_appetite(h[b, t], b, t)
+            if k > 0:
+                b, t = divmod(k - 1, PACK)
+                gather(picked_late[b][:, t, :], h[b, t], pos2_sb)
                 if b == 0:
-                    pick(early[0][:, t, :], h[b, t], pos1_sb)
-                nc.vector.tensor_scalar(lateb[b][:, t, :], lateb[b][:, t, :], late_sb[:, b, t : t + 1], None, ALU.max)
-                if (b, t) == (1, 0):
-                    x2.append(quantize(x2_bf, "x2_0"))
-                    gather(v2_words[1], tab2_sb[1], offs2_sb, 1)
-                if (b, t) == (1, 1):
-                    x1.append(quantize(x1_bf, "x1_0"))
-            x2_bf = round_x(lateb[b], f"x2_bf{b}")
-            if b == 0:
-                x1_bf = round_x(early[0], "x1_bf0")
+                    gather(early[b][:, t, :], h[b, t], pos1_sb)
+            if k == 1:
+                tab2_sb.append(load_words(tab2_words, 1, "tab2_1", AT_C + 1))
+            if k == 3:
+                extra_sb = placed([P, S2 // P, NP], F32, "extra_sb", AT_A - 8)
+                nc.sync.dma_start(extra_sb[:], extra.rearrange("(i p) n -> p i n", p=P))
+            if k in (5, 6):
+                gather(v2_words[k - 5][:], tab2_sb[k - 5], offs2_sb)
+            if k == 7:
+                scaled = placed([P, PACK, NP], F32, "scaled0", AT_D)
+                for t in range(PACK):
+                    times_gain(scaled, 0, t)
+                x1_bf = round_x(scaled, "x1_bf0")
+                x2_bf = [round_x(floor_late(0, placed([P, PACK, NP], F32, "floored0", AT_A + 8)), "x2_bf0")]
+
+        x2_bf.append(round_x(floor_late(1, picked_late[1]), "x2_bf1"))
+        x1.append(quantize(x1_bf, "x1_0"))
 
         tiles = S2 // P
         e2 = [bank(i, f"e2_{i}") for i in range(tiles)]
-        for i in range(tiles):
-            second_stage(e2[i], i, 0, x2[0])
-
-        early.append(keep.tile([P, PACK, NP], F32, name="early1", tag="slot_c", align_bytes=64))
+        early.append(placed([P, PACK, NP], F32, "early1", AT_B + 3))
         for t in range(PACK):
-            pick(early[1][:, t, :], h[1, t], pos1_sb)
-            if t == 1:
-                x2.append(quantize(x2_bf, "x2_1"))
+            gather(early[1][:, t, :], h[1, t], pos1_sb)
+            times_gain(early[1], 1, t)
+            if t == 0:
+                x2.append(quantize(x2_bf[0], "x2_0"))
+                for i in range(tiles):
+                    second_stage(e2[i], i, 0, x2[0])
+        x2.append(quantize(x2_bf[1], "x2_1"))
         for i in range(tiles):
             second_stage(e2[i], i, 1, x2[1])
         x1_bf = round_x(early[1], "x1_bf1")

@@ -19,7 +19,7 @@ PASS = P * PACK
 T, T3, H, S, S2, NP = 4096, 2048, 1024, 1024, 1024, 512
 BANK = 512
 BANKS = 8
-AT_A, AT_B, AT_C, AT_D = 8, 24, 43, 52
+AT_A, AT_B, AT_C, AT_D = 12, 28, 57, 66
 
 FLOPS = 2 * 1024 * H * S + 2 * 2 * H * S2 * NP
 
@@ -73,18 +73,20 @@ def tile_list_breakfast_refill_scores_kernel(
         def bank(i, name):
             return psum.tile([P, BANK], F32, name=name, tag=f"bank{i % BANKS}")
 
-        def quantize(grouped, name):
-            width = grouped.shape[1] // PACK
-            words = keep.tile([P, width], U32, name=f"{name}_words", align_bytes=64)
-            plane = keep.tile([P, width], U8, name=f"{name}_plane", align_bytes=64)
+        def quantize(grouped, name, kib=None):
+            if kib is None:
+                words = keep.tile([P, PASS], U32, name=f"{name}_words", align_bytes=64)
+            else:
+                words = placed([P, PASS], U32, f"{name}_words", kib)
+            plane = keep.tile([P, PASS], U8, name=f"{name}_plane", align_bytes=64)
             nc.vector.quantize_mx(out=words[:].bitcast(E4M3X4), scales=plane[:], in_=grouped[:])
             return words, plane
 
-        def round_w1(b, u):
-            grouped = keep.tile([P, 2 * PASS], BF16, name=f"w1_bf{b}{u}", align_bytes=64)
+        def round_w1(b):
+            grouped = keep.tile([P, PACK * PASS], BF16, name=f"w1_bf{b}", align_bytes=64)
             nc.scalar.copy(
-                grouped[:].rearrange("p (t m j) -> p m t j", t=2, j=PACK),
-                w1_raw[:, b].rearrange("p j (m t) -> p m t j", t=PACK)[:, :, 2 * u : 2 * u + 2, :],
+                grouped[:].rearrange("p (t m j) -> p m t j", t=PACK, j=PACK),
+                w1_raw[:, b].rearrange("p j (m t) -> p m t j", t=PACK),
             )
             return grouped
 
@@ -115,37 +117,38 @@ def tile_list_breakfast_refill_scores_kernel(
         tab2_plane = zeroed(nc.vector, placed([P, T3], U8, "tab2_plane", AT_A - 2))
         load_scale_rows(nc.scalar, tab2_plane, tab2_scales)
 
+        w4_plane = keep.tile([P, H], U8, name="w4_plane", align_bytes=64)
+        nc.gpsimd.tensor_copy(
+            w4_plane[:].rearrange("p (b t m) -> p b t m", b=2, t=PACK),
+            w4_plane_raw[:].rearrange("p (b m t) -> p b t m", b=2, t=PACK),
+        )
+
         v_words = [placed([P, S], U32, f"v{a}", AT_D + 4 * a) for a in range(2)]
         gather(v_words[0][:], tab_sb[0], offs_sb)
         tab_sb.append(load_words(tab_words, 1, "tab1", AT_B + 3))
-        per_row = placed([P, 3, 2, PACK], F32, "per_row", AT_B + 2)
+        per_row = placed([P, 3, 2, PACK], F32, "per_row", AT_B + 1)
         b1_sb, gain_sb, late_sb = [load_per_row(per_row[:, i], vec) for i, vec in enumerate((b1, gain, late))]
         v_plane = placed([P, S], U8, "v_plane", AT_B)
         gather(v_plane[:], tab_plane, offs_sb)
         app = [load_appetite(0, AT_C + 1)]
-        w4_plane = placed([P, H], U8, "w4_plane", AT_B + 1)
-        nc.vector.tensor_copy(
-            w4_plane[:].rearrange("p (b t m) -> p b t m", b=2, t=PACK),
-            w4_plane_raw[:].rearrange("p (b m t) -> p b t m", b=2, t=PACK),
-        )
-        w1_bf = [round_w1(b, u) for b in range(2) for u in range(2)]
+        w1_bf = [round_w1(b) for b in range(2)]
         app.extend(load_appetite(1 + b, AT_A + 8 * b) for b in range(2))
-        w1_q = [quantize(w1_bf[u], f"w1_0{u}") for u in range(2)]
+        w1_q = [quantize(w1_bf[0], "w1_0")]
         v2_plane = placed([P, S2], U8, "v2_plane", AT_C)
         gather(v2_plane[:], tab2_plane, offs2_sb)
-        w1_q.extend(quantize(w1_bf[2 + u], f"w1_1{u}") for u in range(2))
         half_list = offs.shape[1] // 2
         for half in range(2):
             cols = slice(half * BANK, (half + 1) * BANK)
             gather(v_words[1][:, cols], tab_sb[1], offs_sb[:, half * half_list : (half + 1) * half_list])
-        app.append(load_appetite(3, AT_B + 3))
-        tab2_sb = [load_words(tab2_words, 0, "tab2_0", AT_B + 11)]
-        v2_words = [keep.tile([P, S2], U32, name=f"v2_{a}", align_bytes=64) for a in range(2)]
+        app.append(load_appetite(3, AT_B + 12))
+        tab2_sb = [load_words(tab2_words, 0, "tab2_0", AT_B + 4)]
+        w1_q.append(quantize(w1_bf[1], "w1_1", AT_B + 2))
+        v2_words = []
 
         def first_stage(b, t):
             h = keep.tile([P, S], F32, name=f"h{b}{t}")
-            w_words, w_plane = w1_q[2 * b + t // 2]
-            w_cols = slice(t % 2 * P, (t % 2 + 1) * P)
+            w_words, w_plane = w1_q[b]
+            w_cols = slice(t * P, (t + 1) * P)
             c0 = b * PASS + t * P
             for half in range(S // BANK):
                 cols = slice(half * BANK, (half + 1) * BANK)
@@ -165,8 +168,11 @@ def tile_list_breakfast_refill_scores_kernel(
             engine = nc.vector if (b, t) == (0, 0) else nc.gpsimd
             engine.tensor_tensor(h[:], h[:], app[2 * b + t // 2][:, t % 2, :], ALU.mult)
 
-        def round_x(picked, name):
-            grouped = keep.tile([P, PACK * NP], BF16, name=name, align_bytes=64)
+        def round_x(picked, name, kib=None):
+            if kib is None:
+                grouped = keep.tile([P, PACK * NP], BF16, name=name, align_bytes=64)
+            else:
+                grouped = placed([P, PACK * NP], BF16, name, kib)
             nc.scalar.copy(
                 grouped[:].rearrange("p (c i t) -> p c t i", i=4, t=PACK),
                 picked[:].rearrange("p t (c i) -> p c t i", i=4),
@@ -185,8 +191,8 @@ def tile_list_breakfast_refill_scores_kernel(
         picked_late = [keep.tile([P, PACK, NP], F32, name=f"late{b}") for b in range(2)]
         x1, x2 = [], []
 
-        def times_gain(dst, b, t):
-            nc.scalar.activation(dst[:, t, :], early[b][:, t, :], ACT.Copy, scale=gain_sb[:, b, t : t + 1])
+        def times_gain(dst, src, b, t):
+            nc.scalar.activation(dst, src, ACT.Copy, scale=gain_sb[:, b, t : t + 1])
 
         def floor_late(b, dst):
             for t in range(PACK):
@@ -206,33 +212,36 @@ def tile_list_breakfast_refill_scores_kernel(
                 gather(picked_late[b][:, t, :], h[b, t], pos2_sb)
                 if b == 0:
                     gather(early[b][:, t, :], h[b, t], pos1_sb)
+                else:
+                    times_gain(h[b, t][:], h[b, t][:], b, t)
             if k == 1:
                 tab2_sb.append(load_words(tab2_words, 1, "tab2_1", AT_C + 1))
             if k == 3:
-                extra_sb = placed([P, S2 // P, NP], F32, "extra_sb", AT_A - 8)
+                extra_sb = placed([P, S2 // P, NP], F32, "extra_sb", AT_A - 12)
                 nc.sync.dma_start(extra_sb[:], extra.rearrange("(i p) n -> p i n", p=P))
-            if k in (5, 6):
-                gather(v2_words[k - 5][:], tab2_sb[k - 5], offs2_sb)
+            if k in (4, 6):
+                a = len(v2_words)
+                v2_words.append(placed([P, S2], U32, f"v2_{a}", AT_A + 4 + 4 * a))
+                gather(v2_words[a][:], tab2_sb[a], offs2_sb)
             if k == 7:
                 scaled = placed([P, PACK, NP], F32, "scaled0", AT_D)
                 for t in range(PACK):
-                    times_gain(scaled, 0, t)
+                    times_gain(scaled[:, t, :], early[0][:, t, :], 0, t)
                 x1_bf = round_x(scaled, "x1_bf0")
-                x2_bf = [round_x(floor_late(0, placed([P, PACK, NP], F32, "floored0", AT_A + 8)), "x2_bf0")]
 
-        x2_bf.append(round_x(floor_late(1, picked_late[1]), "x2_bf1"))
-        x1.append(quantize(x1_bf, "x1_0"))
+        floored = placed([P, 2, PACK, NP], F32, "floored", AT_B + 3)
+        x2_bf = [round_x(floor_late(0, floored[:, 0]), "x2_bf0", AT_B + 21)]
+        x2_bf.append(round_x(floor_late(1, floored[:, 1]), "x2_bf1"))
+        x1.append(quantize(x1_bf, "x1_0", AT_B + 19))
+        x2.append(quantize(x2_bf[0], "x2_0"))
 
         tiles = S2 // P
         e2 = [bank(i, f"e2_{i}") for i in range(tiles)]
-        early.append(placed([P, PACK, NP], F32, "early1", AT_B + 3))
+        for i in range(tiles):
+            second_stage(e2[i], i, 0, x2[0])
+        early.append(placed([P, PACK, NP], F32, "early1", AT_B + 21))
         for t in range(PACK):
             gather(early[1][:, t, :], h[1, t], pos1_sb)
-            times_gain(early[1], 1, t)
-            if t == 0:
-                x2.append(quantize(x2_bf[0], "x2_0"))
-                for i in range(tiles):
-                    second_stage(e2[i], i, 0, x2[0])
         x2.append(quantize(x2_bf[1], "x2_1"))
         for i in range(tiles):
             second_stage(e2[i], i, 1, x2[1])

@@ -174,8 +174,8 @@ def tile_list_breakfast_refill_scores_kernel(
             else:
                 grouped = placed([P, PACK * NP], BF16, name, kib)
             nc.scalar.copy(
-                grouped[:].rearrange("p (c i t) -> p c t i", i=4, t=PACK),
-                picked[:].rearrange("p t (c i) -> p c t i", i=4),
+                grouped[:].rearrange("p (n t) -> p n t", t=PACK),
+                picked[:].rearrange("p t n -> p n t"),
             )
             return grouped
 
@@ -202,11 +202,10 @@ def tile_list_breakfast_refill_scores_kernel(
                 )
             return dst
 
-        for k in range(2 * PACK + 1):
-            if k < 2 * PACK:
-                b, t = divmod(k, PACK)
-                h[b, t] = first_stage(b, t)
-                times_appetite(h[b, t], b, t)
+        for k in range(2 * PACK):
+            b, t = divmod(k, PACK)
+            h[b, t] = first_stage(b, t)
+            times_appetite(h[b, t], b, t)
             if k > 0:
                 b, t = divmod(k - 1, PACK)
                 gather(picked_late[b][:, t, :], h[b, t], pos2_sb)
@@ -231,7 +230,9 @@ def tile_list_breakfast_refill_scores_kernel(
 
         floored = placed([P, 2, PACK, NP], F32, "floored", AT_B + 3)
         x2_bf = [round_x(floor_late(0, floored[:, 0]), "x2_bf0", AT_B + 21)]
+        gather(picked_late[1][:, PACK - 1, :], h[1, PACK - 1], pos2_sb)
         x2_bf.append(round_x(floor_late(1, floored[:, 1]), "x2_bf1"))
+        times_gain(h[1, PACK - 1][:], h[1, PACK - 1][:], 1, PACK - 1)
         x1.append(quantize(x1_bf, "x1_0", AT_B + 19))
         x2.append(quantize(x2_bf[0], "x2_0"))
 
@@ -241,8 +242,9 @@ def tile_list_breakfast_refill_scores_kernel(
             second_stage(e2[i], i, 0, x2[0])
         early.append(placed([P, PACK, NP], F32, "early1", AT_B + 21))
         for t in range(PACK):
+            if t == PACK - 1:
+                x2.append(quantize(x2_bf[1], "x2_1"))
             gather(early[1][:, t, :], h[1, t], pos1_sb)
-        x2.append(quantize(x2_bf[1], "x2_1"))
         for i in range(tiles):
             second_stage(e2[i], i, 1, x2[1])
         x1_bf = round_x(early[1], "x1_bf1")

@@ -16,12 +16,37 @@ ACT = mybir.ActivationFunctionType
 P = 128
 PACK = 4
 PASS = P * PACK
+PASSES = 2
+QUADRANTS, QUADRANT = 4, 32
 T, T3, H, S, S2, NP = 4096, 2048, 1024, 1024, 1024, 512
 BANK = 512
-BANKS = 8
-AT_A, AT_B, AT_C, AT_D = 12, 28, 57, 66
+FIRST_STAGE_BANKS = 4
 
-FLOPS = 2 * 1024 * H * S + 2 * 2 * H * S2 * NP
+EXTRA_FIRST = 5
+
+FLOPS = 2 * PASSES * PASS * H * S + 2 * 2 * H * S2 * NP
+
+AT_W4_RAW = 11
+AT_TAB2_PLANE = 10
+AT_W1_RAW = 12
+AT_TAB = (28, 30)
+AT_V_PLANE = 28
+AT_B1 = 29
+AT_W1_BF = (74, 78)
+AT_GAIN_LATE = 74
+AT_TAB_PLANE = 57
+AT_V2_PLANE = 57
+AT_V = (66, 70)
+AT_W1_PLANE_1 = 30
+AT_APPETITE = (58, 12, 20, 40)
+AT_TAB2 = (31, 58)
+AT_EXTRA = (3, 21)
+AT_X1_PLANE_1 = 3
+AT_V2 = (13, 17)
+AT_X1_GAINED = 66
+AT_FLOORED = 30
+AT_X1_PLANE_0 = 46
+AT_LAST = 47
 
 
 def tile_list_breakfast_refill_scores_kernel(
@@ -35,8 +60,14 @@ def tile_list_breakfast_refill_scores_kernel(
         arena = ctx.enter_context(tc.tile_pool(name="arena", bufs=1))
         psum = ctx.enter_context(tc.psum_pool(name="psum", bufs=1))
 
+        def kept(shape, dtype, name):
+            return keep.tile(shape, dtype, name=name, align_bytes=64)
+
         def placed(shape, dtype, name, kib):
             return arena.tile(shape, dtype, name=name, offset=kib * 1024, align_bytes=64)
+
+        def bank(i, name):
+            return psum.tile([P, BANK], F32, name=name, tag=f"bank{i}")
 
         def load_list(src, name):
             tile = lists.tile(list(src.shape), U16, name=name)
@@ -49,214 +80,207 @@ def tile_list_breakfast_refill_scores_kernel(
 
         def load_scale_rows(queue, plane, scales):
             passes = scales.shape[0]
-            for q in range(4):
+            for q in range(QUADRANTS):
                 rows = scales[:, 4 * q : 4 * q + 4, :] if passes > 1 else scales[0, 4 * q : 4 * q + 4, :]
-                queue.dma_start(plane[32 * q : 32 * q + 4 * passes, :].bitcast(I32), rows.bitcast(I32))
+                queue.dma_start(plane[QUADRANT * q : QUADRANT * q + 4 * passes, :].bitcast(I32), rows.bitcast(I32))
 
         def load_words(words, a, name, kib):
             tile = placed([P, words.shape[2]], U32, name, kib)
             nc.sync.dma_start(tile[:].bitcast(I32), words[a].rearrange("p t i -> p (t i)").bitcast(I32))
             return tile
 
-
-        def load_appetite(pair, kib):
-            b, t0 = pair // 2, 2 * (pair % 2)
-            tile = placed([P, 2, S], F32, f"app{pair}", kib)
+        def load_appetite(pair):
+            b, t0 = divmod(2 * pair, PACK)
+            tile = placed([P, 2, S], F32, f"appetite{pair}", AT_APPETITE[pair])
             rows = appetite[b * PASS : (b + 1) * PASS, :].rearrange("(p t) j -> p t j", t=PACK)
             nc.sync.dma_start(tile[:], rows[:, t0 : t0 + 2, :])
             return tile
+
+        def load_extra(part, first, end):
+            tile = placed([P, end - first, NP], F32, f"extra{part}", AT_EXTRA[part])
+            nc.sync.dma_start(tile[:], extra[first * P : end * P, :].rearrange("(i p) n -> p i n", p=P))
+            return [tile[:, i, :] for i in range(end - first)]
 
         def load_per_row(dst, vec):
             nc.sync.dma_start(dst, vec.rearrange("(b p t) -> p b t", p=P, t=PACK))
             return dst
 
-        def bank(i, name):
-            return psum.tile([P, BANK], F32, name=name, tag=f"bank{i % BANKS}")
+        def gather(dst, window, offsets):
+            nc.vector.tensor_copy(dst, window[:].indirect(offsets[:]))
 
-        def quantize(grouped, name, kib=None):
-            if kib is None:
-                words = keep.tile([P, PASS], U32, name=f"{name}_words", align_bytes=64)
-            else:
-                words = placed([P, PASS], U32, f"{name}_words", kib)
-            plane = keep.tile([P, PASS], U8, name=f"{name}_plane", align_bytes=64)
-            nc.vector.quantize_mx(out=words[:].bitcast(E4M3X4), scales=plane[:], in_=grouped[:])
+        def deal(engine, dst, src):
+            engine.tensor_copy(
+                dst.rearrange("p (b t m) -> p b t m", b=PASSES, t=PACK),
+                src.rearrange("p (b m t) -> p b t m", b=PASSES, t=PACK),
+            )
+
+        def quantize(grouped, name, plane):
+            words = kept([P, PASS], U32, f"{name}_words")
+            nc.vector.quantize_mx(out=words[:].bitcast(E4M3X4), scales=plane[:], in_=grouped)
             return words, plane
 
+        tab_plane = zeroed(nc.vector, placed([P, T], U8, "tab_plane", AT_TAB_PLANE))
+        w4_plane_raw = zeroed(nc.gpsimd, kept([P, H], U8, "w4_plane_raw"))
+
+        offs_sb = load_list(offs, "offs_sb")
+        w4_raw = placed([P, 2 * H], U8, "w4_raw", AT_W4_RAW)
+        nc.sync.dma_start(w4_raw[:].bitcast(I32), w4_words[0].bitcast(I32))
+        offs2_sb = load_list(offs2, "offs2_sb")
+        pos2_sb = load_list(pos2, "pos2_sb")
+        pos1_sb = load_list(pos1, "pos1_sb")
+        tab_sb = [load_words(tab_words, 0, "tab0", AT_TAB[0])]
+        load_scale_rows(nc.scalar, tab_plane, tab_scales)
+        load_scale_rows(nc.gpsimd, w4_plane_raw, w4_scales)
+
+        w4 = kept([P, H], U16, "w4")
+        deal(nc.vector, w4[:], w4_raw[:].bitcast(U16))
+        w1_raw = placed([P, PASSES, PACK, PASS], F32, "w1_raw", AT_W1_RAW)
+        for b in range(PASSES):
+            nc.sync.dma_start(w1_raw[:, b], w1[:, b * PASS : (b + 1) * PASS].rearrange("(p j) c -> p j c", j=PACK))
+        tab2_plane = zeroed(nc.vector, placed([P, T3], U8, "tab2_plane", AT_TAB2_PLANE))
+        load_scale_rows(nc.scalar, tab2_plane, tab2_scales)
+        w4_plane = kept([P, H], U8, "w4_plane")
+        deal(nc.gpsimd, w4_plane[:], w4_plane_raw[:])
+
         def round_w1(b):
-            grouped = keep.tile([P, PACK * PASS], BF16, name=f"w1_bf{b}", align_bytes=64)
+            grouped = placed([P, PACK * PASS], BF16, f"w1_bf{b}", AT_W1_BF[b])
             nc.scalar.copy(
                 grouped[:].rearrange("p (t m j) -> p m t j", t=PACK, j=PACK),
                 w1_raw[:, b].rearrange("p j (m t) -> p m t j", t=PACK),
             )
             return grouped
 
-        def gather(dst, window, offsets):
-            nc.vector.tensor_copy(dst, window[:].indirect(offsets[:]))
-
-        tab_plane = zeroed(nc.vector, placed([P, T], U8, "tab_plane", AT_C))
-        w4_plane_raw = zeroed(nc.gpsimd, keep.tile([P, H], U8, name="w4_plane_raw", align_bytes=64))
-
-        offs_sb = load_list(offs, "offs_sb")
-        w4_raw = placed([P, 2 * H], U8, "w4_raw", AT_A - 1)
-        nc.sync.dma_start(w4_raw[:].bitcast(I32), w4_words[0].bitcast(I32))
-        offs2_sb = load_list(offs2, "offs2_sb")
-        pos2_sb = load_list(pos2, "pos2_sb")
-        pos1_sb = load_list(pos1, "pos1_sb")
-        tab_sb = [load_words(tab_words, 0, "tab0", AT_B)]
-        load_scale_rows(nc.scalar, tab_plane, tab_scales)
-        load_scale_rows(nc.gpsimd, w4_plane_raw, w4_scales)
-
-        w4 = keep.tile([P, H], U16, name="w4", align_bytes=64)
-        nc.vector.tensor_copy(
-            w4[:].rearrange("p (b t m) -> p b t m", b=2, t=PACK),
-            w4_raw[:].bitcast(U16).rearrange("p (b m t) -> p b t m", b=2, t=PACK),
-        )
-        w1_raw = placed([P, 2, PACK, PASS], F32, "w1_raw", AT_A)
-        for b in range(2):
-            nc.sync.dma_start(w1_raw[:, b], w1[:, b * PASS : (b + 1) * PASS].rearrange("(p j) c -> p j c", j=PACK))
-        tab2_plane = zeroed(nc.vector, placed([P, T3], U8, "tab2_plane", AT_A - 2))
-        load_scale_rows(nc.scalar, tab2_plane, tab2_scales)
-
-        w4_plane = keep.tile([P, H], U8, name="w4_plane", align_bytes=64)
-        nc.gpsimd.tensor_copy(
-            w4_plane[:].rearrange("p (b t m) -> p b t m", b=2, t=PACK),
-            w4_plane_raw[:].rearrange("p (b m t) -> p b t m", b=2, t=PACK),
-        )
-
-        v_words = [placed([P, S], U32, f"v{a}", AT_D + 4 * a) for a in range(2)]
+        v_words = [placed([P, S], U32, f"v{a}", AT_V[a]) for a in range(PASSES)]
         gather(v_words[0][:], tab_sb[0], offs_sb)
-        tab_sb.append(load_words(tab_words, 1, "tab1", AT_B + 3))
-        per_row = placed([P, 3, 2, PACK], F32, "per_row", AT_B + 1)
-        b1_sb, gain_sb, late_sb = [load_per_row(per_row[:, i], vec) for i, vec in enumerate((b1, gain, late))]
-        v_plane = placed([P, S], U8, "v_plane", AT_B)
+        tab_sb.append(load_words(tab_words, 1, "tab1", AT_TAB[1]))
+        b1_sb = load_per_row(placed([P, PASSES, PACK], F32, "b1_sb", AT_B1)[:], b1)
+        v_plane = placed([P, S], U8, "v_plane", AT_V_PLANE)
         gather(v_plane[:], tab_plane, offs_sb)
-        app = [load_appetite(0, AT_C + 1)]
-        w1_bf = [round_w1(b) for b in range(2)]
-        app.extend(load_appetite(1 + b, AT_A + 8 * b) for b in range(2))
-        w1_q = [quantize(w1_bf[0], "w1_0")]
-        v2_plane = placed([P, S2], U8, "v2_plane", AT_C)
+        appetite_sb = [load_appetite(0)]
+        w1_bf = [round_w1(b) for b in range(PASSES)]
+        appetite_sb.extend(load_appetite(pair) for pair in (1, 2))
+        w1_q = [quantize(w1_bf[0][:], "w1_0", kept([P, PASS], U8, "w1_0_plane"))]
+        gain_late = placed([P, 2, PASSES, PACK], F32, "gain_late", AT_GAIN_LATE)
+        gain_sb, late_sb = [load_per_row(gain_late[:, i], vec) for i, vec in enumerate((gain, late))]
+        v2_plane = placed([P, S2], U8, "v2_plane", AT_V2_PLANE)
         gather(v2_plane[:], tab2_plane, offs2_sb)
         half_list = offs.shape[1] // 2
         for half in range(2):
             cols = slice(half * BANK, (half + 1) * BANK)
             gather(v_words[1][:, cols], tab_sb[1], offs_sb[:, half * half_list : (half + 1) * half_list])
-        app.append(load_appetite(3, AT_B + 12))
-        tab2_sb = [load_words(tab2_words, 0, "tab2_0", AT_B + 4)]
-        w1_q.append(quantize(w1_bf[1], "w1_1", AT_B + 2))
-        v2_words = []
+        appetite_sb.append(load_appetite(3))
+        tab2_sb = [load_words(tab2_words, 0, "tab2_0", AT_TAB2[0])]
+        w1_q.append(quantize(w1_bf[1][:], "w1_1", placed([P, PASS], U8, "w1_1_plane", AT_W1_PLANE_1)))
 
         def first_stage(b, t):
-            h = keep.tile([P, S], F32, name=f"h{b}{t}")
-            w_words, w_plane = w1_q[b]
-            w_cols = slice(t * P, (t + 1) * P)
-            c0 = b * PASS + t * P
+            tile = PACK * b + t
+            rows = kept([P, S], F32, f"h{tile}")
+            w1_words, w1_plane = w1_q[b]
+            w1_cols = slice(t * P, (t + 1) * P)
+            w4_cols = slice(tile * P, (tile + 1) * P)
             for half in range(S // BANK):
                 cols = slice(half * BANK, (half + 1) * BANK)
-                y = bank(2 * (PACK * b + t) + half, f"y{b}{t}{half}")
+                y = bank((2 * tile + half) % FIRST_STAGE_BANKS, f"y{tile}_{half}")
                 nc.tensor.matmul_mx(
-                    y[:], lhsT=w4[:, c0 : c0 + P].bitcast(E2M1X4), lhsT_scale=w4_plane[:, c0 : c0 + P],
+                    y[:], lhsT=w4[:, w4_cols].bitcast(E2M1X4), lhsT_scale=w4_plane[:, w4_cols],
                     rhs=v_words[0][:, cols].bitcast(E4M3X4), rhs_scale=v_plane[:, cols], start=True, stop=False,
                 )
                 nc.tensor.matmul_mx(
-                    y[:], lhsT=w_words[:, w_cols].bitcast(E4M3X4), lhsT_scale=w_plane[:, w_cols],
+                    y[:], lhsT=w1_words[:, w1_cols].bitcast(E4M3X4), lhsT_scale=w1_plane[:, w1_cols],
                     rhs=v_words[1][:, cols].bitcast(E4M3X4), rhs_scale=v_plane[4:P, cols], start=False, stop=True,
                 )
-                nc.scalar.activation(h[:, cols], y[:], ACT.Tanh, bias=b1_sb[:, b, t : t + 1])
-            return h
-
-        def times_appetite(h, b, t):
-            engine = nc.vector if (b, t) == (0, 0) else nc.gpsimd
-            engine.tensor_tensor(h[:], h[:], app[2 * b + t // 2][:, t % 2, :], ALU.mult)
-
-        def round_x(picked, name, kib=None):
-            if kib is None:
-                grouped = keep.tile([P, PACK * NP], BF16, name=name, align_bytes=64)
-            else:
-                grouped = placed([P, PACK * NP], BF16, name, kib)
-            nc.scalar.copy(
-                grouped[:].rearrange("p (n t) -> p n t", t=PACK),
-                picked[:].rearrange("p t n -> p n t"),
-            )
-            return grouped
-
-        def second_stage(acc, i, a, x):
-            nc.tensor.matmul_mx(
-                acc[:], lhsT=v2_words[a][:, i * P : (i + 1) * P].bitcast(E4M3X4),
-                lhsT_scale=v2_plane[4 * a : P, i * P : (i + 1) * P],
-                rhs=x[0][:].bitcast(E4M3X4), rhs_scale=x[1][:], start=(a == 0), stop=(a == 1),
-            )
-
-        h = {}
-        early = [keep.tile([P, PACK, NP], F32, name="early0")]
-        picked_late = [keep.tile([P, PACK, NP], F32, name=f"late{b}") for b in range(2)]
-        x1, x2 = [], []
+                nc.scalar.activation(rows[:, cols], y[:], ACT.Tanh, bias=b1_sb[:, b, t : t + 1])
+            engine = nc.vector if tile == 0 else nc.gpsimd
+            engine.tensor_tensor(rows[:], rows[:], appetite_sb[tile // 2][:, tile % 2, :], ALU.mult)
+            return rows
 
         def times_gain(dst, src, b, t):
             nc.scalar.activation(dst, src, ACT.Copy, scale=gain_sb[:, b, t : t + 1])
 
-        def floor_late(b, dst):
+        def round_x(grouped, picked):
+            nc.scalar.copy(grouped.rearrange("p (n t) -> p n t", t=PACK), picked.rearrange("p t n -> p n t"))
+            return grouped
+
+        h = {}
+        picked1 = kept([P, PACK, NP], F32, "picked1")
+        picked2 = [kept([P, PACK, NP], F32, f"picked2_{b}") for b in range(PASSES)]
+        v2_words = []
+
+        def pick(b, t):
+            gather(picked2[b][:, t, :], h[b, t], pos2_sb)
+            if b == 0:
+                gather(picked1[:, t, :], h[b, t], pos1_sb)
+            else:
+                times_gain(h[b, t][:], h[b, t][:], b, t)
+
+        def gather_v2(a):
+            v2_words.append(placed([P, S2], U32, f"v2_{a}", AT_V2[a]))
+            gather(v2_words[a][:], tab2_sb[a], offs2_sb)
+
+        row_tiles = [(b, t) for b in range(PASSES) for t in range(PACK)]
+        for tile, (b, t) in enumerate(row_tiles):
+            h[b, t] = first_stage(b, t)
+            if tile > 0:
+                pick(*row_tiles[tile - 1])
+            if tile == 1:
+                tab2_sb.append(load_words(tab2_words, 1, "tab2_1", AT_TAB2[1]))
+            if tile == 3:
+                extra_sb = load_extra(0, 0, EXTRA_FIRST)
+            if tile == 5:
+                extra_sb.extend(load_extra(1, EXTRA_FIRST, S2 // P))
+            if tile == 4:
+                gather_v2(0)
+            if tile == 6:
+                gather_v2(1)
+        x1_gained = placed([P, PACK, NP], F32, "x1_gained", AT_X1_GAINED)
+        for t in range(PACK):
+            times_gain(x1_gained[:, t, :], picked1[:, t, :], 0, t)
+        x1_bf = [round_x(kept([P, PACK * NP], BF16, "x1_bf0")[:], x1_gained[:])]
+        pick(*row_tiles[-1])
+
+        floored = placed([P, PASSES * PACK * NP], F32, "floored", AT_FLOORED)
+        last = placed([P, (PACK + 1) * NP], F32, "last", AT_LAST)
+        x2_bf = []
+        for b in range(PASSES):
+            x2_rows = floored[:, b * PACK * NP : (b + 1) * PACK * NP].rearrange("p (t n) -> p t n", t=PACK)
             for t in range(PACK):
                 nc.vector.tensor_scalar(
-                    dst[:, t, :], picked_late[b][:, t, :], gain_sb[:, b, t : t + 1], late_sb[:, b, t : t + 1],
+                    x2_rows[:, t, :], picked2[b][:, t, :], gain_sb[:, b, t : t + 1], late_sb[:, b, t : t + 1],
                     ALU.mult, ALU.max,
                 )
-            return dst
+            x2_bf.append(round_x(last[:, (1 + 2 * b) * NP : (3 + 2 * b) * NP].bitcast(BF16), x2_rows))
+        x1 = [quantize(x1_bf[0], "x1_0", placed([P, NP], U8, "x1_0_plane", AT_X1_PLANE_0))]
 
-        for k in range(2 * PACK):
-            b, t = divmod(k, PACK)
-            h[b, t] = first_stage(b, t)
-            times_appetite(h[b, t], b, t)
-            if k > 0:
-                b, t = divmod(k - 1, PACK)
-                gather(picked_late[b][:, t, :], h[b, t], pos2_sb)
-                if b == 0:
-                    gather(early[b][:, t, :], h[b, t], pos1_sb)
-                else:
-                    times_gain(h[b, t][:], h[b, t][:], b, t)
-            if k == 1:
-                tab2_sb.append(load_words(tab2_words, 1, "tab2_1", AT_C + 1))
-            if k == 3:
-                extra_sb = placed([P, S2 // P, NP], F32, "extra_sb", AT_A - 12)
-                nc.sync.dma_start(extra_sb[:], extra.rearrange("(i p) n -> p i n", p=P))
-            if k in (4, 6):
-                a = len(v2_words)
-                v2_words.append(placed([P, S2], U32, f"v2_{a}", AT_A + 4 + 4 * a))
-                gather(v2_words[a][:], tab2_sb[a], offs2_sb)
-            if k == 7:
-                scaled = placed([P, PACK, NP], F32, "scaled0", AT_D)
-                for t in range(PACK):
-                    times_gain(scaled[:, t, :], early[0][:, t, :], 0, t)
-                x1_bf = round_x(scaled, "x1_bf0")
+        def second_stage(acc, i, a, x):
+            dishes = slice(i * P, (i + 1) * P)
+            words, plane = x
+            nc.tensor.matmul_mx(
+                acc[:], lhsT=v2_words[a][:, dishes].bitcast(E4M3X4), lhsT_scale=v2_plane[4 * a : P, dishes],
+                rhs=words[:].bitcast(E4M3X4), rhs_scale=plane[:], start=(a == 0), stop=(a == PASSES - 1),
+            )
 
-        floored = placed([P, 2, PACK, NP], F32, "floored", AT_B + 3)
-        x2_bf = [round_x(floor_late(0, floored[:, 0]), "x2_bf0", AT_B + 21)]
-        gather(picked_late[1][:, PACK - 1, :], h[1, PACK - 1], pos2_sb)
-        x2_bf.append(round_x(floor_late(1, floored[:, 1]), "x2_bf1"))
-        times_gain(h[1, PACK - 1][:], h[1, PACK - 1][:], 1, PACK - 1)
-        x1.append(quantize(x1_bf, "x1_0", AT_B + 19))
-        x2.append(quantize(x2_bf[0], "x2_0"))
-
-        tiles = S2 // P
-        e2 = [bank(i, f"e2_{i}") for i in range(tiles)]
-        for i in range(tiles):
-            second_stage(e2[i], i, 0, x2[0])
-        early.append(placed([P, PACK, NP], F32, "early1", AT_B + 21))
+        dish_tiles = range(S2 // P)
+        e2 = [bank(i, f"e2_{i}") for i in dish_tiles]
         for t in range(PACK):
-            if t == PACK - 1:
-                x2.append(quantize(x2_bf[1], "x2_1"))
-            gather(early[1][:, t, :], h[1, t], pos1_sb)
-        for i in range(tiles):
-            second_stage(e2[i], i, 1, x2[1])
-        x1_bf = round_x(early[1], "x1_bf1")
+            if t % 2 == 1:
+                a = t // 2
+                x2 = quantize(x2_bf[a], f"x2_{a}", kept([P, NP], U8, f"x2_{a}_plane"))
+                for i in dish_tiles:
+                    second_stage(e2[i], i, a, x2)
+            gather(last[:, t * NP : (t + 1) * NP], h[1, t], pos1_sb)
+        x1_rows = last[:, : PACK * NP].rearrange("p (t n) -> p t n", t=PACK)
+        x1_bf.append(round_x(kept([P, PACK * NP], BF16, "x1_bf1")[:], x1_rows))
+
+        scores = kept([P, S2 // P, NP], F32, "scores")
         e1 = []
-        for i in range(tiles):
-            nc.vector.tensor_tensor(extra_sb[:, i, :], e2[i][:], extra_sb[:, i, :], ALU.add)
+        for i in dish_tiles:
+            nc.vector.tensor_tensor(scores[:, i, :], e2[i][:], extra_sb[i], ALU.add)
             e1.append(bank(i, f"e1_{i}"))
             second_stage(e1[i], i, 0, x1[0])
-            if i == 4:
-                x1.append(quantize(x1_bf, "x1_1"))
-        for i in range(tiles):
+            if i == EXTRA_FIRST - 1:
+                x1.append(quantize(x1_bf[1], "x1_1", placed([P, NP], U8, "x1_1_plane", AT_X1_PLANE_1)))
+        for i in dish_tiles:
             second_stage(e1[i], i, 1, x1[1])
-        for i in range(tiles):
-            nc.vector.tensor_tensor(extra_sb[:, i, :], e1[i][:], extra_sb[:, i, :], ALU.max)
-            nc.sync.dma_start(out[i * P : (i + 1) * P, :], extra_sb[:, i, :])
+        for i in dish_tiles:
+            nc.vector.tensor_tensor(scores[:, i, :], e1[i][:], scores[:, i, :], ALU.max)
+            nc.sync.dma_start(out[i * P : (i + 1) * P, :], scores[:, i, :])

from contextlib import ExitStack

import concourse.mybir as mybir

F32 = mybir.dt.float32
BF16 = mybir.dt.bfloat16
I32 = mybir.dt.int32
U32 = mybir.dt.uint32
U16 = mybir.dt.uint16
U8 = mybir.dt.uint8
E4M3X4 = mybir.dt.float8_e4m3fn_x4
E2M1X4 = mybir.dt.float4_e2m1fn_x4
ALU = mybir.AluOpType
ACT = mybir.ActivationFunctionType

P = 128
PACK = 4
PASS = P * PACK
PASSES = 2
QUADRANTS, QUADRANT = 4, 32
T, T3, H, S, S2, NP = 4096, 2048, 1024, 1024, 1024, 512
BANK = 512
FIRST_STAGE_BANKS = 4

EXTRA_FIRST = 5

FLOPS = 2 * PASSES * PASS * H * S + 2 * 2 * H * S2 * NP

AT_W4_RAW = 11
AT_TAB2_PLANE = 10
AT_W1_RAW = 12
AT_TAB = (28, 30)
AT_V_PLANE = 28
AT_B1 = 29
AT_W1_BF = (74, 78)
AT_GAIN_LATE = 74
AT_TAB_PLANE = 57
AT_V2_PLANE = 57
AT_V = (66, 70)
AT_W1_PLANE_1 = 30
AT_APPETITE = (58, 12, 20, 40)
AT_TAB2 = (31, 58)
AT_EXTRA = (3, 21)
AT_X1_PLANE_1 = 3
AT_V2 = (13, 17)
AT_X1_GAINED = 66
AT_FLOORED = 30
AT_X1_PLANE_0 = 46
AT_LAST = 47


def tile_list_breakfast_refill_scores_kernel(
    tc, tab_words, tab_scales, offs, tab2_words, tab2_scales, offs2, pos1, pos2,
    w4_words, w4_scales, w1, b1, appetite, gain, late, extra, out,
):
    nc = tc.nc
    with ExitStack() as ctx:
        lists = ctx.enter_context(tc.tile_pool(name="lists", bufs=1))
        keep = ctx.enter_context(tc.tile_pool(name="keep", bufs=1))
        arena = ctx.enter_context(tc.tile_pool(name="arena", bufs=1))
        psum = ctx.enter_context(tc.psum_pool(name="psum", bufs=1))

        def kept(shape, dtype, name):
            return keep.tile(shape, dtype, name=name, align_bytes=64)

        def placed(shape, dtype, name, kib):
            return arena.tile(shape, dtype, name=name, offset=kib * 1024, align_bytes=64)

        def bank(i, name):
            return psum.tile([P, BANK], F32, name=name, tag=f"bank{i}")

        def load_list(src, name):
            tile = lists.tile(list(src.shape), U16, name=name)
            nc.sync.dma_start(tile[:], src)
            return tile

        def zeroed(engine, plane):
            engine.memset(plane[:].bitcast(I32), 0)
            return plane

        def load_scale_rows(queue, plane, scales):
            passes = scales.shape[0]
            for q in range(QUADRANTS):
                rows = scales[:, 4 * q : 4 * q + 4, :] if passes > 1 else scales[0, 4 * q : 4 * q + 4, :]
                queue.dma_start(plane[QUADRANT * q : QUADRANT * q + 4 * passes, :].bitcast(I32), rows.bitcast(I32))

        def load_words(words, a, name, kib):
            tile = placed([P, words.shape[2]], U32, name, kib)
            nc.sync.dma_start(tile[:].bitcast(I32), words[a].rearrange("p t i -> p (t i)").bitcast(I32))
            return tile

        def load_appetite(pair):
            b, t0 = divmod(2 * pair, PACK)
            tile = placed([P, 2, S], F32, f"appetite{pair}", AT_APPETITE[pair])
            rows = appetite[b * PASS : (b + 1) * PASS, :].rearrange("(p t) j -> p t j", t=PACK)
            nc.sync.dma_start(tile[:], rows[:, t0 : t0 + 2, :])
            return tile

        def load_extra(part, first, end):
            tile = placed([P, end - first, NP], F32, f"extra{part}", AT_EXTRA[part])
            nc.sync.dma_start(tile[:], extra[first * P : end * P, :].rearrange("(i p) n -> p i n", p=P))
            return [tile[:, i, :] for i in range(end - first)]

        def load_per_row(dst, vec):
            nc.sync.dma_start(dst, vec.rearrange("(b p t) -> p b t", p=P, t=PACK))
            return dst

        def gather(dst, window, offsets):
            nc.vector.tensor_copy(dst, window[:].indirect(offsets[:]))

        def deal(engine, dst, src):
            engine.tensor_copy(
                dst.rearrange("p (b t m) -> p b t m", b=PASSES, t=PACK),
                src.rearrange("p (b m t) -> p b t m", b=PASSES, t=PACK),
            )

        def quantize(grouped, name, plane):
            words = kept([P, PASS], U32, f"{name}_words")
            nc.vector.quantize_mx(out=words[:].bitcast(E4M3X4), scales=plane[:], in_=grouped)
            return words, plane

        tab_plane = zeroed(nc.vector, placed([P, T], U8, "tab_plane", AT_TAB_PLANE))
        w4_plane_raw = zeroed(nc.gpsimd, kept([P, H], U8, "w4_plane_raw"))

        offs_sb = load_list(offs, "offs_sb")
        w4_raw = placed([P, 2 * H], U8, "w4_raw", AT_W4_RAW)
        nc.sync.dma_start(w4_raw[:].bitcast(I32), w4_words[0].bitcast(I32))
        offs2_sb = load_list(offs2, "offs2_sb")
        pos2_sb = load_list(pos2, "pos2_sb")
        pos1_sb = load_list(pos1, "pos1_sb")
        tab_sb = [load_words(tab_words, 0, "tab0", AT_TAB[0])]
        load_scale_rows(nc.scalar, tab_plane, tab_scales)
        load_scale_rows(nc.gpsimd, w4_plane_raw, w4_scales)

        w4 = kept([P, H], U16, "w4")
        deal(nc.vector, w4[:], w4_raw[:].bitcast(U16))
        w1_raw = placed([P, PASSES, PACK, PASS], F32, "w1_raw", AT_W1_RAW)
        for b in range(PASSES):
            nc.sync.dma_start(w1_raw[:, b], w1[:, b * PASS : (b + 1) * PASS].rearrange("(p j) c -> p j c", j=PACK))
        tab2_plane = zeroed(nc.vector, placed([P, T3], U8, "tab2_plane", AT_TAB2_PLANE))
        load_scale_rows(nc.scalar, tab2_plane, tab2_scales)
        w4_plane = kept([P, H], U8, "w4_plane")
        deal(nc.gpsimd, w4_plane[:], w4_plane_raw[:])

        def round_w1(b):
            grouped = placed([P, PACK * PASS], BF16, f"w1_bf{b}", AT_W1_BF[b])
            nc.scalar.copy(
                grouped[:].rearrange("p (t m j) -> p m t j", t=PACK, j=PACK),
                w1_raw[:, b].rearrange("p j (m t) -> p m t j", t=PACK),
            )
            return grouped

        v_words = [placed([P, S], U32, f"v{a}", AT_V[a]) for a in range(PASSES)]
        gather(v_words[0][:], tab_sb[0], offs_sb)
        tab_sb.append(load_words(tab_words, 1, "tab1", AT_TAB[1]))
        b1_sb = load_per_row(placed([P, PASSES, PACK], F32, "b1_sb", AT_B1)[:], b1)
        v_plane = placed([P, S], U8, "v_plane", AT_V_PLANE)
        gather(v_plane[:], tab_plane, offs_sb)
        appetite_sb = [load_appetite(0)]
        w1_bf = [round_w1(b) for b in range(PASSES)]
        appetite_sb.extend(load_appetite(pair) for pair in (1, 2))
        w1_q = [quantize(w1_bf[0][:], "w1_0", kept([P, PASS], U8, "w1_0_plane"))]
        gain_late = placed([P, 2, PASSES, PACK], F32, "gain_late", AT_GAIN_LATE)
        gain_sb, late_sb = [load_per_row(gain_late[:, i], vec) for i, vec in enumerate((gain, late))]
        v2_plane = placed([P, S2], U8, "v2_plane", AT_V2_PLANE)
        gather(v2_plane[:], tab2_plane, offs2_sb)
        half_list = offs.shape[1] // 2
        for half in range(2):
            cols = slice(half * BANK, (half + 1) * BANK)
            gather(v_words[1][:, cols], tab_sb[1], offs_sb[:, half * half_list : (half + 1) * half_list])
        appetite_sb.append(load_appetite(3))
        tab2_sb = [load_words(tab2_words, 0, "tab2_0", AT_TAB2[0])]
        w1_q.append(quantize(w1_bf[1][:], "w1_1", placed([P, PASS], U8, "w1_1_plane", AT_W1_PLANE_1)))

        def first_stage(b, t):
            tile = PACK * b + t
            rows = kept([P, S], F32, f"h{tile}")
            w1_words, w1_plane = w1_q[b]
            w1_cols = slice(t * P, (t + 1) * P)
            w4_cols = slice(tile * P, (tile + 1) * P)
            for half in range(S // BANK):
                cols = slice(half * BANK, (half + 1) * BANK)
                y = bank((2 * tile + half) % FIRST_STAGE_BANKS, f"y{tile}_{half}")
                nc.tensor.matmul_mx(
                    y[:], lhsT=w4[:, w4_cols].bitcast(E2M1X4), lhsT_scale=w4_plane[:, w4_cols],
                    rhs=v_words[0][:, cols].bitcast(E4M3X4), rhs_scale=v_plane[:, cols], start=True, stop=False,
                )
                nc.tensor.matmul_mx(
                    y[:], lhsT=w1_words[:, w1_cols].bitcast(E4M3X4), lhsT_scale=w1_plane[:, w1_cols],
                    rhs=v_words[1][:, cols].bitcast(E4M3X4), rhs_scale=v_plane[4:P, cols], start=False, stop=True,
                )
                nc.scalar.activation(rows[:, cols], y[:], ACT.Tanh, bias=b1_sb[:, b, t : t + 1])
            engine = nc.vector if tile == 0 else nc.gpsimd
            engine.tensor_tensor(rows[:], rows[:], appetite_sb[tile // 2][:, tile % 2, :], ALU.mult)
            return rows

        def times_gain(dst, src, b, t):
            nc.scalar.activation(dst, src, ACT.Copy, scale=gain_sb[:, b, t : t + 1])

        def round_x(grouped, picked):
            nc.scalar.copy(grouped.rearrange("p (n t) -> p n t", t=PACK), picked.rearrange("p t n -> p n t"))
            return grouped

        h = {}
        picked1 = kept([P, PACK, NP], F32, "picked1")
        picked2 = [kept([P, PACK, NP], F32, f"picked2_{b}") for b in range(PASSES)]
        v2_words = []

        def pick(b, t):
            gather(picked2[b][:, t, :], h[b, t], pos2_sb)
            if b == 0:
                gather(picked1[:, t, :], h[b, t], pos1_sb)
            else:
                times_gain(h[b, t][:], h[b, t][:], b, t)

        def gather_v2(a):
            v2_words.append(placed([P, S2], U32, f"v2_{a}", AT_V2[a]))
            gather(v2_words[a][:], tab2_sb[a], offs2_sb)

        row_tiles = [(b, t) for b in range(PASSES) for t in range(PACK)]
        for tile, (b, t) in enumerate(row_tiles):
            h[b, t] = first_stage(b, t)
            if tile > 0:
                pick(*row_tiles[tile - 1])
            if tile == 1:
                tab2_sb.append(load_words(tab2_words, 1, "tab2_1", AT_TAB2[1]))
            if tile == 3:
                extra_sb = load_extra(0, 0, EXTRA_FIRST)
            if tile == 5:
                extra_sb.extend(load_extra(1, EXTRA_FIRST, S2 // P))
            if tile == 4:
                gather_v2(0)
            if tile == 6:
                gather_v2(1)
        x1_gained = placed([P, PACK, NP], F32, "x1_gained", AT_X1_GAINED)
        for t in range(PACK):
            times_gain(x1_gained[:, t, :], picked1[:, t, :], 0, t)
        x1_bf = [round_x(kept([P, PACK * NP], BF16, "x1_bf0")[:], x1_gained[:])]
        pick(*row_tiles[-1])

        floored = placed([P, PASSES * PACK * NP], F32, "floored", AT_FLOORED)
        last = placed([P, (PACK + 1) * NP], F32, "last", AT_LAST)
        x2_bf = []
        for b in range(PASSES):
            x2_rows = floored[:, b * PACK * NP : (b + 1) * PACK * NP].rearrange("p (t n) -> p t n", t=PACK)
            for t in range(PACK):
                nc.vector.tensor_scalar(
                    x2_rows[:, t, :], picked2[b][:, t, :], gain_sb[:, b, t : t + 1], late_sb[:, b, t : t + 1],
                    ALU.mult, ALU.max,
                )
            x2_bf.append(round_x(last[:, (1 + 2 * b) * NP : (3 + 2 * b) * NP].bitcast(BF16), x2_rows))
        x1 = [quantize(x1_bf[0], "x1_0", placed([P, NP], U8, "x1_0_plane", AT_X1_PLANE_0))]

        def second_stage(acc, i, a, x):
            dishes = slice(i * P, (i + 1) * P)
            words, plane = x
            nc.tensor.matmul_mx(
                acc[:], lhsT=v2_words[a][:, dishes].bitcast(E4M3X4), lhsT_scale=v2_plane[4 * a : P, dishes],
                rhs=words[:].bitcast(E4M3X4), rhs_scale=plane[:], start=(a == 0), stop=(a == PASSES - 1),
            )

        dish_tiles = range(S2 // P)
        e2 = [bank(i, f"e2_{i}") for i in dish_tiles]
        for t in range(PACK):
            if t % 2 == 1:
                a = t // 2
                x2 = quantize(x2_bf[a], f"x2_{a}", kept([P, NP], U8, f"x2_{a}_plane"))
                for i in dish_tiles:
                    second_stage(e2[i], i, a, x2)
            gather(last[:, t * NP : (t + 1) * NP], h[1, t], pos1_sb)
        x1_rows = last[:, : PACK * NP].rearrange("p (t n) -> p t n", t=PACK)
        x1_bf.append(round_x(kept([P, PACK * NP], BF16, "x1_bf1")[:], x1_rows))

        scores = kept([P, S2 // P, NP], F32, "scores")
        e1 = []
        for i in dish_tiles:
            nc.vector.tensor_tensor(scores[:, i, :], e2[i][:], extra_sb[i], ALU.add)
            e1.append(bank(i, f"e1_{i}"))
            second_stage(e1[i], i, 0, x1[0])
            if i == EXTRA_FIRST - 1:
                x1.append(quantize(x1_bf[1], "x1_1", placed([P, NP], U8, "x1_1_plane", AT_X1_PLANE_1)))
        for i in dish_tiles:
            second_stage(e1[i], i, 1, x1[1])
        for i in dish_tiles:
            nc.vector.tensor_tensor(scores[:, i, :], e1[i][:], scores[:, i, :], ALU.max)
            nc.sync.dma_start(out[i * P : (i + 1) * P, :], scores[:, i, :])
